import numpy as np
import ml_dtypes

BF16 = ml_dtypes.bfloat16


def bf(x):
    return np.asarray(x, np.float32).astype(BF16)


def f32(x):
    return np.asarray(x, np.float32)


def f64(x):
    return np.asarray(x).astype(np.float64)


def striped(idx):
    return np.tile(idx.reshape(-1, 16).T, (8, 1))


S, A, K, M, N, E, Q = 512, 256, 128, 512, 384, 2, 192


def setup_inputs():
    return {"x": bf(np.random.standard_normal((A, S))), "wd": bf(np.random.standard_normal((A, M)) / np.sqrt(A)), "y": bf(np.random.standard_normal((K, N))), "w": bf(np.random.standard_normal((E, K, M)) / np.sqrt(K)), "b": f32(0.5 * np.random.standard_normal((M, 1))), "offs": striped(np.random.permutation(S)[:N])}


def reference(x, wd, y, w, b, offs):
    idx = offs[:16].T.reshape(-1)
    z = f64(wd).T @ f64(x)
    for e in range(E):
        z[:, idx[e * Q : (e + 1) * Q]] += f64(w)[e].T @ f64(y)[:, e * Q : (e + 1) * Q]
    return np.tanh(z + f64(b))

@@ -1,0 +1,56 @@
+import concourse.mybir as mybir
+
+BF16, F32, U16 = mybir.dt.bfloat16, mybir.dt.float32, mybir.dt.uint16
+TANH = mybir.ActivationFunctionType.Tanh
+
+P = 128
+S, A, K, M, N, E = 512, 256, 128, 512, 384, 2
+Q = N // E
+PER_COLUMN = 16
+
+FLOPS = 2 * A * M * S + 2 * K * M * N
+
+
+def tile_rows_fillproj_tanh_kernel(tc, x, wd, y, w, b, offs, out):
+    nc = tc.nc
+    depth_blocks = A // P
+    row_blocks = M // P
+    with (
+        tc.tile_pool(name="held", bufs=1) as held,
+        tc.psum_pool(name="psum", bufs=1) as psum,
+    ):
+        x_sb = held.tile([P, depth_blocks, S], BF16)
+        nc.sync.dma_start(x_sb[:], x.rearrange("(p k) s -> p k s", k=depth_blocks))
+        wd_sb = held.tile([P, depth_blocks, M], BF16)
+        nc.sync.dma_start(wd_sb[:], wd.rearrange("(p k) m -> p k m", k=depth_blocks))
+        offsets = held.tile([P, N // PER_COLUMN], U16)
+        nc.sync.dma_start(offsets[:], offs)
+        y_sb = held.tile([P, N], BF16)
+        nc.sync.dma_start(y_sb[:], y)
+        w_sb = held.tile([P, E, M], BF16)
+        nc.sync.dma_start(w_sb[:], w.rearrange("e k m -> k e m"))
+        bias = held.tile([P, row_blocks], F32)
+        nc.sync.dma_start(bias[:], b.rearrange("(a p) o -> p (a o)", p=P))
+
+        windows = [psum.tile([P, S], F32, name=f"window{a}") for a in range(row_blocks)]
+        for a in range(row_blocks):
+            for k in range(depth_blocks):
+                nc.tensor.matmul(
+                    windows[a][:], wd_sb[:, k, a * P : (a + 1) * P], x_sb[:, k, :], start=k == 0, stop=False
+                )
+
+        columns = Q // PER_COLUMN
+        for a in range(row_blocks):
+            for e in range(E):
+                nc.tensor.matmul(
+                    windows[a][:].indirect(offsets[:, e * columns : (e + 1) * columns]),
+                    w_sb[:, e, a * P : (a + 1) * P],
+                    y_sb[:, e * Q : (e + 1) * Q],
+                    start=False,
+                    stop=e == E - 1,
+                )
+
+        for a in range(row_blocks):
+            result = held.tile([P, S], F32, name=f"result{a}")
+            nc.scalar.activation(result[:], windows[a][:], TANH, bias=bias[:, a : a + 1])
+            nc.sync.dma_start(out[a * P : (a + 1) * P, :], result[:])

@@ -7,6 +7,7 @@ P = 128
 S, A, K, M, N, E = 512, 256, 128, 512, 384, 2
 Q = N // E
 PER_COLUMN = 16
+WARM_UPS = 5
 
 FLOPS = 2 * A * M * S + 2 * K * M * N
 
@@ -19,6 +20,14 @@ def tile_rows_fillproj_tanh_kernel(tc, x, wd, y, w, b, offs, out):
         tc.tile_pool(name="held", bufs=1) as held,
         tc.psum_pool(name="psum", bufs=1) as psum,
     ):
+        zeros = held.tile([P, S], BF16)
+        nc.vector.memset(zeros[:], 0.0)
+        spare_bank = psum.tile([P, S], F32)
+        for i in range(WARM_UPS):
+            nc.tensor.matmul(spare_bank[:], zeros[:, 0:P], zeros[:], start=True, stop=True)
+        spare_tanh = held.tile([P, 1], F32)
+        nc.scalar.activation(spare_tanh[:], zeros[:, 0:1], TANH)
+
         x_sb = held.tile([P, depth_blocks, S], BF16)
         nc.sync.dma_start(x_sb[:], x.rearrange("(p k) s -> p k s", k=depth_blocks))
         wd_sb = held.tile([P, depth_blocks, M], BF16)

@@ -28,10 +28,14 @@ def tile_rows_fillproj_tanh_kernel(tc, x, wd, y, w, b, offs, out):
         spare_tanh = held.tile([P, 1], F32)
         nc.scalar.activation(spare_tanh[:], zeros[:, 0:1], TANH)
 
-        x_sb = held.tile([P, depth_blocks, S], BF16)
-        nc.sync.dma_start(x_sb[:], x.rearrange("(p k) s -> p k s", k=depth_blocks))
-        wd_sb = held.tile([P, depth_blocks, M], BF16)
-        nc.sync.dma_start(wd_sb[:], wd.rearrange("(p k) m -> p k m", k=depth_blocks))
+        x_sb, wd_sb = [], []
+        for k in range(depth_blocks):
+            x_block = held.tile([P, S], BF16, name=f"x{k}")
+            nc.sync.dma_start(x_block[:], x[k * P : (k + 1) * P, :])
+            x_sb.append(x_block)
+            wd_block = held.tile([P, M], BF16, name=f"wd{k}")
+            nc.sync.dma_start(wd_block[:], wd[k * P : (k + 1) * P, :])
+            wd_sb.append(wd_block)
         offsets = held.tile([P, N // PER_COLUMN], U16)
         nc.sync.dma_start(offsets[:], offs)
         y_sb = held.tile([P, N], BF16)
@@ -39,27 +43,26 @@ def tile_rows_fillproj_tanh_kernel(tc, x, wd, y, w, b, offs, out):
         w_sb = held.tile([P, E, M], BF16)
         nc.sync.dma_start(w_sb[:], w.rearrange("e k m -> k e m"))
         bias = held.tile([P, row_blocks], F32)
-        nc.sync.dma_start(bias[:], b.rearrange("(a p) o -> p (a o)", p=P))
+        nc.sync.dma_start(bias[:], b.rearrange("(p a) o -> p (a o)", a=row_blocks))
 
         windows = [psum.tile([P, S], F32, name=f"window{a}") for a in range(row_blocks)]
-        for a in range(row_blocks):
-            for k in range(depth_blocks):
-                nc.tensor.matmul(
-                    windows[a][:], wd_sb[:, k, a * P : (a + 1) * P], x_sb[:, k, :], start=k == 0, stop=False
-                )
+        for k in range(depth_blocks):
+            for a in range(row_blocks):
+                nc.tensor.matmul(windows[a][:], wd_sb[k][:, a::row_blocks], x_sb[k][:], start=k == 0, stop=False)
 
         columns = Q // PER_COLUMN
         for a in range(row_blocks):
             for e in range(E):
                 nc.tensor.matmul(
                     windows[a][:].indirect(offsets[:, e * columns : (e + 1) * columns]),
-                    w_sb[:, e, a * P : (a + 1) * P],
+                    w_sb[:, e, a::row_blocks],
                     y_sb[:, e * Q : (e + 1) * Q],
                     start=False,
                     stop=e == E - 1,
                 )
 
+        out_rows = out.rearrange("(p a) s -> p a s", a=row_blocks)
         for a in range(row_blocks):
             result = held.tile([P, S], F32, name=f"result{a}")
             nc.scalar.activation(result[:], windows[a][:], TANH, bias=bias[:, a : a + 1])
-            nc.sync.dma_start(out[a * P : (a + 1) * P, :], result[:])
+            nc.sync.dma_start(out_rows[:, a, :], result[:])

@@ -7,7 +7,7 @@ P = 128
 S, A, K, M, N, E = 512, 256, 128, 512, 384, 2
 Q = N // E
 PER_COLUMN = 16
-WARM_UPS = 5
+WARM_UPS = 3
 
 FLOPS = 2 * A * M * S + 2 * K * M * N
 

import concourse.mybir as mybir

BF16, F32, U16 = mybir.dt.bfloat16, mybir.dt.float32, mybir.dt.uint16
TANH = mybir.ActivationFunctionType.Tanh

P = 128
S, A, K, M, N, E = 512, 256, 128, 512, 384, 2
Q = N // E
PER_COLUMN = 16
WARM_UPS = 3

FLOPS = 2 * A * M * S + 2 * K * M * N


def tile_rows_fillproj_tanh_kernel(tc, x, wd, y, w, b, offs, out):
    nc = tc.nc
    depth_blocks = A // P
    row_blocks = M // P
    with (
        tc.tile_pool(name="held", bufs=1) as held,
        tc.psum_pool(name="psum", bufs=1) as psum,
    ):
        zeros = held.tile([P, S], BF16)
        nc.vector.memset(zeros[:], 0.0)
        spare_bank = psum.tile([P, S], F32)
        for i in range(WARM_UPS):
            nc.tensor.matmul(spare_bank[:], zeros[:, 0:P], zeros[:], start=True, stop=True)
        spare_tanh = held.tile([P, 1], F32)
        nc.scalar.activation(spare_tanh[:], zeros[:, 0:1], TANH)

        x_sb, wd_sb = [], []
        for k in range(depth_blocks):
            x_block = held.tile([P, S], BF16, name=f"x{k}")
            nc.sync.dma_start(x_block[:], x[k * P : (k + 1) * P, :])
            x_sb.append(x_block)
            wd_block = held.tile([P, M], BF16, name=f"wd{k}")
            nc.sync.dma_start(wd_block[:], wd[k * P : (k + 1) * P, :])
            wd_sb.append(wd_block)
        offsets = held.tile([P, N // PER_COLUMN], U16)
        nc.sync.dma_start(offsets[:], offs)
        y_sb = held.tile([P, N], BF16)
        nc.sync.dma_start(y_sb[:], y)
        w_sb = held.tile([P, E, M], BF16)
        nc.sync.dma_start(w_sb[:], w.rearrange("e k m -> k e m"))
        bias = held.tile([P, row_blocks], F32)
        nc.sync.dma_start(bias[:], b.rearrange("(p a) o -> p (a o)", a=row_blocks))

        windows = [psum.tile([P, S], F32, name=f"window{a}") for a in range(row_blocks)]
        for k in range(depth_blocks):
            for a in range(row_blocks):
                nc.tensor.matmul(windows[a][:], wd_sb[k][:, a::row_blocks], x_sb[k][:], start=k == 0, stop=False)

        columns = Q // PER_COLUMN
        for a in range(row_blocks):
            for e in range(E):
                nc.tensor.matmul(
                    windows[a][:].indirect(offsets[:, e * columns : (e + 1) * columns]),
                    w_sb[:, e, a::row_blocks],
                    y_sb[:, e * Q : (e + 1) * Q],
                    start=False,
                    stop=e == E - 1,
                )

        out_rows = out.rearrange("(p a) s -> p a s", a=row_blocks)
        for a in range(row_blocks):
            result = held.tile([P, S], F32, name=f"result{a}")
            nc.scalar.activation(result[:], windows[a][:], TANH, bias=bias[:, a : a + 1])
            nc.sync.dma_start(out_rows[:, a, :], result[:])
